import numpy as np
import ml_dtypes


def mxq(x, axis, fmt="e4m3"):
    dtype, down = {"e4m3": (ml_dtypes.float8_e4m3fn, 7), "e5m2": (ml_dtypes.float8_e5m2, 14)}[fmt]
    v = np.moveaxis(np.asarray(x, np.float32).astype(ml_dtypes.bfloat16).astype(np.float64), axis, -1)
    blocks = v.reshape(v.shape[:-1] + (-1, 32))
    amax = np.abs(blocks).max(-1, keepdims=True)
    byte = np.maximum(np.where(amax > 0, np.frexp(amax)[1] - 1 + 127, 0) - down, 1)
    scale = np.exp2(byte - 127.0)
    codes = (blocks / scale).astype(np.float32).astype(dtype).astype(np.float64)
    return np.moveaxis((codes * scale).reshape(v.shape), -1, axis)


WIDE = False


def mx_kscale(k):
    if not WIDE:
        return np.ones(k)
    levels = np.array([10, -10, 5, -5, 0])
    if k % 512:
        return np.exp2(np.random.permutation(np.resize(levels, k // 32))).repeat(32)
    a = np.empty((k // 512, 16))
    for p in range(k // 512):
        a[p, :8] = np.random.permutation(np.resize(levels, 8))
        for g in range(8):
            far = levels[np.abs(levels - a[p, g]) >= 10]
            a[p, g + 8] = far[np.random.randint(len(far))]
    return np.exp2(a.ravel()).repeat(32)


def f64(x):
    return np.asarray(x).astype(np.float64)


def striped(idx):
    return np.tile(idx.reshape(-1, 16).T, (8, 1)).astype(np.uint16)


def unstriped(offs):
    return offs[:16].T.reshape(-1).astype(np.int64)


def striped8(idx):
    return np.concatenate([x.reshape(-1, 16).T for x in idx]).astype(np.uint16)


def runs(offs, k):
    lists = np.stack([offs[16 * r : 16 * r + 16].T.reshape(-1) for r in range(8)]).astype(np.int64)
    return lists[np.arange(k) % 512 // 64]


def pack_weight(w):
    k, n = w.shape
    w = f64(np.asarray(w, np.float32).astype(ml_dtypes.bfloat16)).reshape(k // 32, 32, n)
    amax = np.abs(w).max(1)
    byte = np.clip(np.where(amax > 0, np.frexp(amax)[1] - 1 + 127 - 7, 1), 1, 254)
    scaled = (w * np.exp2(127.0 - byte)[:, None, :]).reshape(k, n).astype(np.float32)
    words = np.ascontiguousarray(scaled.reshape(k // 512, 128, 4, n).transpose(0, 1, 3, 2)).astype(ml_dtypes.float8_e4m3fn).view(np.uint8)
    return words, np.ascontiguousarray(byte.astype(np.uint8).reshape(k // 512, 16, n))


def unpack_weight(words, scales):
    g, p, n, _ = words.shape
    vals = np.ascontiguousarray(words).view(ml_dtypes.float8_e4m3fn).astype(np.float64) * np.repeat(np.exp2(scales.astype(np.float64) - 127.0), 8, axis=1)[..., None]
    return vals.transpose(0, 1, 3, 2).reshape(g * 512, n)


def sigmoid(v):
    return 1.0 / (1.0 + np.exp(-np.maximum(v, -700.0)))


K, T, S, N, H, G = 512, 2048, 512, 512, 512, 2048


def setup_inputs():
    n = np.random.standard_normal
    s = mx_kscale(K)[:, None]
    u = mx_kscale(S)
    packed_xT = pack_weight(n((K, T)) * s)
    packed_dT = pack_weight(n((K, G)) / s)
    return {
        "x_words": packed_xT[0],
        "x_scales": packed_xT[1],
        "w1": (n((K, H)) / np.sqrt(K) / s).astype(np.float32),
        "gn": (np.random.uniform(0.5, 1.5, (H, 1)) * u[:, None]).astype(np.float32),
        "w2": (n((H, N)) / np.sqrt(H) / u[:, None]).astype(np.float32),
        "d_words": packed_dT[0],
        "d_scales": packed_dT[1],
        "offs": striped(np.random.permutation(T)[:S]),
        "n1": striped8(np.stack([np.random.permutation(S) for _ in range(8)])),
        "n2": striped8(np.stack([np.random.permutation(S) for _ in range(8)])),
        "two": striped(np.random.permutation(T)[:S]),
        "k1": striped8(np.random.randint(0, G, (8, H))),
        "n3": striped(np.random.permutation(S)),
        "n4": striped(np.random.permutation(S)),
    }


def reference(x_words, x_scales, w1, gn, w2, d_words, d_scales, offs, n1, n2, two, k1, n3, n4):
    xq = unpack_weight(x_words, x_scales)[:, unstriped(offs)]
    y = mxq(f64(w1), 0, "e4m3").T @ xq
    z = f64(gn) * (np.maximum(y[np.arange(H)[:, None], runs(n1, H)], y[np.arange(H)[:, None], runs(n2, H)]) - (0.75 * y))
    a = mxq(f64(w2), 0, "e4m3").T @ mxq(z, 0, "e4m3")
    d_k1 = unpack_weight(d_words, d_scales)[np.arange(K)[:, None], runs(k1, K)]
    x_two = unpack_weight(x_words, x_scales)[:, unstriped(two)]
    b = 0.0625 * (d_k1.T @ x_two)
    return a * (sigmoid(b[:, unstriped(n4)])) - (0.5 * a[:, unstriped(n3)])

@@ -1,0 +1,190 @@
+from contextlib import ExitStack
+
+import concourse.mybir as mybir
+
+K, T, S, N, H, G = 512, 2048, 512, 512, 512, 2048
+FLOPS = 3 * 2 * 512 * 512 * 512
+
+F32 = mybir.dt.float32
+BF16 = mybir.dt.bfloat16
+I32 = mybir.dt.int32
+U32 = mybir.dt.uint32
+U16 = mybir.dt.uint16
+U8 = mybir.dt.uint8
+FP8X4 = mybir.dt.float8_e4m3fn_x4
+ALU = mybir.AluOpType
+ACT = mybir.ActivationFunctionType
+
+P = 128
+PACK = 4
+HALF = S // 2
+LIST_COLS = S // 16
+
+
+def tile_picked_cdjoingatebover_none_p_kernel(
+    tc, x_words, x_scales, w1, gn, w2, d_words, d_scales, offs, n1, n2, two, k1, n3, n4, out
+):
+    nc = tc.nc
+    with ExitStack() as ctx:
+        keep = ctx.enter_context(tc.tile_pool(name="keep", bufs=1))
+        psum = ctx.enter_context(tc.psum_pool(name="psum", bufs=1))
+
+        def tile(name, shape, dtype, tag=None):
+            return keep.tile(shape, dtype, name=name, tag=tag or name, align_bytes=64)
+
+        def load_list(name, src):
+            held = tile(name, [P, LIST_COLS], U16)
+            nc.sync.dma_start(held[:], src)
+            return held
+
+        def cols(h):
+            return slice(h * HALF, (h + 1) * HALF)
+
+        def entries(held, h):
+            return held[:, h * HALF // 16 : (h + 1) * HALF // 16]
+
+        def mx(acc, lhs_w, lhs_s, rhs_w, rhs_s):
+            nc.tensor.matmul_mx(out=acc, lhsT=lhs_w.bitcast(FP8X4), lhsT_scale=lhs_s,
+                                rhs=rhs_w.bitcast(FP8X4), rhs_scale=rhs_s, start=True, stop=True)
+
+        xs = tile("xs", [P, T], U8)
+        ds = tile("ds", [P, G], U8)
+        dk_s = tile("dk_s", [P, H], U8)
+        xs_in = tile("xs_in", [P, T], U8)
+        nc.vector.memset(xs[:].bitcast(I32), 0)
+        nc.vector.memset(ds[:].bitcast(I32), 0)
+        nc.vector.memset(dk_s[:].bitcast(I32), 0)
+
+        l_offs = load_list("l_offs", offs)
+        for q in range(4):
+            nc.sync.dma_start(xs_in[32 * q : 32 * q + 4, :].bitcast(I32), x_scales[0, 4 * q : 4 * q + 4, :].bitcast(I32))
+        w1_raw = tile("w1_raw", [P, PACK, H], F32)
+        nc.sync.dma_start(w1_raw[:], w1.rearrange("(p j) c -> p j c", j=PACK))
+        xw = tile("xw", [P, T], U32)
+        nc.sync.dma_start(xw[:].bitcast(I32), x_words[0].rearrange("p n t -> p (n t)").bitcast(I32))
+        l_two = load_list("l_two", two)
+        l_k1 = load_list("l_k1", k1)
+        nc.gpsimd.dma_start(ds[0:P:8, :].bitcast(I32), d_scales[0].bitcast(I32))
+        l_n1 = load_list("l_n1", n1)
+        l_n2 = load_list("l_n2", n2)
+        gain = tile("gain", [P, PACK], F32)
+        nc.gpsimd.dma_start(gain[:], gn.rearrange("(p t) o -> p (t o)", t=PACK))
+        l_n4 = load_list("l_n4", n4)
+        l_n3 = load_list("l_n3", n3)
+        dw = tile("dw", [P, G], U32)
+        nc.sync.dma_start(dw[:].bitcast(I32), d_words[0].rearrange("p n t -> p (n t)").bitcast(I32))
+        w2_raw = tile("w2_raw", [P, PACK, N], F32)
+        nc.sync.dma_start(w2_raw[:], w2.rearrange("(p j) c -> p j c", j=PACK))
+
+        for q in range(4):
+            nc.vector.tensor_copy(xs[32 * q : 32 * q + 4, :].bitcast(I32), xs_in[32 * q : 32 * q + 4, :].bitcast(I32))
+        xq_s = tile("xq_s", [P, S], U8)
+        nc.vector.tensor_copy(xq_s[:], xs[:].indirect(l_offs[:]))
+        w1_bf = tile("w1_bf", [P, PACK * P * PACK], BF16)
+        w1_dst = w1_bf[:].rearrange("p (t m j) -> p m j t", t=PACK, j=PACK)
+        w1_src = w1_raw[:].rearrange("p j (m t) -> p m j t", t=PACK)
+        nc.scalar.copy(w1_dst[:, : P // 2], w1_src[:, : P // 2])
+        nc.vector.tensor_copy(w1_dst[:, P // 2 :], w1_src[:, P // 2 :])
+        w1_w = tile("w1_w", [P, H], U32)
+        w1_s = tile("w1_s", [P, H], U8)
+        nc.vector.quantize_mx(out=w1_w[:].bitcast(FP8X4), scales=w1_s[:], in_=w1_bf[:])
+        xq_w = tile("xq_w", [P, S], U32)
+        nc.vector.tensor_copy(xq_w[:], xw[:].indirect(l_offs[:]))
+        y_sb = []
+        for t in range(PACK):
+            acc = psum.tile([P, S], F32, name="acc_y%d" % t, tag="bank%d" % t)
+            rows = slice(t * P, (t + 1) * P)
+            mx(acc[:], w1_w[:, rows], w1_s[:, rows], xq_w[:], xq_s[:])
+            y_t = tile("y%d" % t, [P, S], F32)
+            nc.scalar.copy(y_t[:], acc[:])
+            y_sb.append(y_t)
+
+        x2_s = tile("x2_s", [P, S], U8)
+        nc.vector.tensor_copy(x2_s[:], xs[:].indirect(l_two[:]))
+        dk_g = tile("dk_g", [P, H], U8)
+        nc.vector.tensor_copy(dk_g[:], ds[:].indirect(l_k1[:]))
+        for q in range(4):
+            nc.sync.dma_start(dk_s[32 * q : 32 * q + 4, :].bitcast(I32), dk_g[32 * q : 32 * q + 32 : 8, :].bitcast(I32))
+        x2_w = tile("x2_w", [P, S], U32)
+        nc.vector.tensor_copy(x2_w[:], xw[:].indirect(l_two[:]))
+        dk_w = tile("dk_w", [P, H], U32)
+        nc.vector.tensor_copy(dk_w[:], dw[:].indirect(l_k1[:]))
+        b_acc = []
+        for t in range(PACK):
+            acc = psum.tile([P, S], F32, name="acc_b%d" % t, tag="bank%d" % (PACK + t))
+            rows = slice(t * P, (t + 1) * P)
+            mx(acc[:], dk_w[:, rows], dk_s[:, rows], x2_w[:], x2_s[:])
+            b_acc.append(acc)
+
+        w2_w = tile("w2_w", [P, N], U32)
+        w2_s = tile("w2_s", [P, N], U8)
+
+        def quantise_w2():
+            w2_bf = tile("w2_bf", [P, N * PACK], BF16)
+            nc.vector.tensor_copy(w2_bf[:].rearrange("p (c i j) -> p c j i", i=4, j=PACK),
+                                  w2_raw[:].rearrange("p j (c i) -> p c j i", i=4))
+            nc.vector.quantize_mx(out=w2_w[:].bitcast(FP8X4), scales=w2_s[:], in_=w2_bf[:])
+
+        th = [tile("th%d" % t, [P, S], F32) for t in range(PACK)]
+        a_half = [tile("a_half%d" % t, [P, S], F32) for t in range(PACK)]
+
+        def make_z(h):
+            at1 = tile("at1_%d" % h, [P, PACK, HALF], F32)
+            at2 = tile("at2_%d" % h, [P, PACK, HALF], F32)
+            top = tile("top_%d" % h, [P, PACK, HALF], F32, tag="w2_raw" if h == 0 else None)
+            u = tile("u_%d" % h, [P, PACK, HALF], F32)
+            for t in range(PACK):
+                nc.scalar.activation(at1[:, t, :], y_sb[t][:].indirect(entries(l_n1, h)), ACT.Copy)
+                nc.scalar.activation(at2[:, t, :], y_sb[t][:].indirect(entries(l_n2, h)), ACT.Copy)
+                nc.vector.tensor_tensor(top[:, t, :], at1[:, t, :], at2[:, t, :], ALU.max)
+                nc.vector.scalar_tensor_tensor(u[:, t, :], y_sb[t][:, cols(h)], -0.75, top[:, t, :], ALU.mult, ALU.add)
+            z_bf = tile("z_bf%d" % h, [P, HALF * PACK], BF16)
+            nc.vector.tensor_tensor(
+                z_bf[:].rearrange("p (c i t) -> p c t i", i=4, t=PACK),
+                u[:].rearrange("p t (c i) -> p c t i", i=4),
+                gain[:].unsqueeze(1).unsqueeze(3).broadcast_to([P, HALF // 4, PACK, 4]),
+                ALU.mult,
+            )
+            z_w = tile("z_w%d" % h, [P, HALF], U32)
+            z_s = tile("z_s%d" % h, [P, HALF], U8)
+            nc.vector.quantize_mx(out=z_w[:].bitcast(FP8X4), scales=z_s[:], in_=z_bf[:])
+            return z_w, z_s
+
+        def make_a(h, z_w, z_s):
+            for pair in range(2):
+                acc = psum.tile([P, 2, HALF], F32, name="acc_a%d_%d" % (h, pair), tag="bank%d" % (2 * h + pair))
+                for e in range(2):
+                    rows = slice((2 * pair + e) * P, (2 * pair + e + 1) * P)
+                    mx(acc[:, e, :], w2_w[:, rows], w2_s[:, rows], z_w[:], z_s[:])
+                for e in range(2):
+                    nc.scalar.activation(a_half[2 * pair + e][:, cols(h)], acc[:, e, :], ACT.Copy, scale=-0.5)
+
+        quantise_w2()
+        z0 = make_z(0)
+        z1 = make_z(1)
+        for t in range(PACK):
+            nc.scalar.activation(th[t][:], b_acc[t][:], ACT.Tanh, scale=0.03125)
+        make_a(0, *z0)
+        make_a(1, *z1)
+        th4_first = tile("th4_first", [P, S], F32, tag="top_1")
+        th4_rest = tile("th4_rest", [P, PACK - 1, S], F32, tag="z_w1")
+        for t in range(PACK):
+            th4 = th4_first[:] if t == 0 else th4_rest[:, t - 1, :]
+            for h in range(2):
+                if t == 0:
+                    nc.vector.tensor_copy(th4[:, cols(h)], th[t][:].indirect(entries(l_n4, h)))
+                else:
+                    nc.scalar.activation(th4[:, cols(h)], th[t][:].indirect(entries(l_n4, h)), ACT.Copy)
+            neg = tile("neg%d" % t, [P, S], F32)
+            nc.vector.scalar_tensor_tensor(neg[:], th4, 1.0, a_half[t][:], ALU.add, ALU.mult)
+            res = tile("res%d" % t, [P, S], F32)
+            if t < PACK - 1:
+                for h in range(2):
+                    nc.vector.tensor_tensor(res[:, cols(h)], a_half[t][:].indirect(entries(l_n3, h)), neg[:, cols(h)], ALU.subtract)
+                nc.sync.dma_start(out[t * P : (t + 1) * P, :], res[:])
+            else:
+                at3 = tile("at3", [P, S], F32)
+                for h in range(2):
+                    nc.scalar.activation(at3[:, cols(h)], a_half[t][:].indirect(entries(l_n3, h)), ACT.Copy)
+                    nc.vector.tensor_tensor(res[:, cols(h)], at3[:, cols(h)], neg[:, cols(h)], ALU.subtract)
+                    nc.sync.dma_start(out[t * P : (t + 1) * P, cols(h)], res[:, cols(h)])

@@ -19,6 +19,8 @@ P = 128
 PACK = 4
 HALF = S // 2
 LIST_COLS = S // 16
+S_WINDOW = S + 16
+V_WINDOW = S + 192
 
 
 def tile_picked_cdjoingatebover_none_p_kernel(
@@ -51,9 +53,17 @@ def tile_picked_cdjoingatebover_none_p_kernel(
         ds = tile("ds", [P, G], U8)
         dk_s = tile("dk_s", [P, H], U8)
         xs_in = tile("xs_in", [P, T], U8)
-        nc.vector.memset(xs[:].bitcast(I32), 0)
         nc.vector.memset(ds[:].bitcast(I32), 0)
+        nc.vector.memset(xs[:].bitcast(I32), 0)
+        nc.gpsimd.dma_start(ds[0:P:8, :].bitcast(I32), d_scales[0].bitcast(I32))
         nc.vector.memset(dk_s[:].bitcast(I32), 0)
+        y_sb = [tile("y%d" % t, [P, 2 * S], F32) for t in range(PACK)]
+        th = [tile("th%d" % t, [P, V_WINDOW if t == 0 else S_WINDOW], F32) for t in range(PACK)]
+        a_half = [tile("a_half%d" % t, [P, S_WINDOW], F32) for t in range(PACK)]
+        for window in y_sb:
+            nc.vector.memset(window[:, S:], 0.0)
+        for window in th + a_half:
+            nc.gpsimd.memset(window[:, S:], 0.0)
 
         l_offs = load_list("l_offs", offs)
         for q in range(4):
@@ -64,17 +74,16 @@ def tile_picked_cdjoingatebover_none_p_kernel(
         nc.sync.dma_start(xw[:].bitcast(I32), x_words[0].rearrange("p n t -> p (n t)").bitcast(I32))
         l_two = load_list("l_two", two)
         l_k1 = load_list("l_k1", k1)
-        nc.gpsimd.dma_start(ds[0:P:8, :].bitcast(I32), d_scales[0].bitcast(I32))
         l_n1 = load_list("l_n1", n1)
         l_n2 = load_list("l_n2", n2)
-        gain = tile("gain", [P, PACK], F32)
-        nc.gpsimd.dma_start(gain[:], gn.rearrange("(p t) o -> p (t o)", t=PACK))
         l_n4 = load_list("l_n4", n4)
         l_n3 = load_list("l_n3", n3)
         dw = tile("dw", [P, G], U32)
         nc.sync.dma_start(dw[:].bitcast(I32), d_words[0].rearrange("p n t -> p (n t)").bitcast(I32))
         w2_raw = tile("w2_raw", [P, PACK, N], F32)
         nc.sync.dma_start(w2_raw[:], w2.rearrange("(p j) c -> p j c", j=PACK))
+        gain = tile("gain", [P, PACK], F32)
+        nc.sync.dma_start(gain[:], gn.rearrange("(p t) o -> p (t o)", t=PACK))
 
         for q in range(4):
             nc.vector.tensor_copy(xs[32 * q : 32 * q + 4, :].bitcast(I32), xs_in[32 * q : 32 * q + 4, :].bitcast(I32))
@@ -90,14 +99,11 @@ def tile_picked_cdjoingatebover_none_p_kernel(
         nc.vector.quantize_mx(out=w1_w[:].bitcast(FP8X4), scales=w1_s[:], in_=w1_bf[:])
         xq_w = tile("xq_w", [P, S], U32)
         nc.vector.tensor_copy(xq_w[:], xw[:].indirect(l_offs[:]))
-        y_sb = []
         for t in range(PACK):
             acc = psum.tile([P, S], F32, name="acc_y%d" % t, tag="bank%d" % t)
             rows = slice(t * P, (t + 1) * P)
             mx(acc[:], w1_w[:, rows], w1_s[:, rows], xq_w[:], xq_s[:])
-            y_t = tile("y%d" % t, [P, S], F32)
-            nc.scalar.copy(y_t[:], acc[:])
-            y_sb.append(y_t)
+            nc.scalar.copy(y_sb[t][:, :S], acc[:])
 
         x2_s = tile("x2_s", [P, S], U8)
         nc.vector.tensor_copy(x2_s[:], xs[:].indirect(l_two[:]))
@@ -116,75 +122,102 @@ def tile_picked_cdjoingatebover_none_p_kernel(
             mx(acc[:], dk_w[:, rows], dk_s[:, rows], x2_w[:], x2_s[:])
             b_acc.append(acc)
 
+        w2_bf = tile("w2_bf", [P, N * PACK], BF16)
+        nc.vector.tensor_copy(w2_bf[:].rearrange("p (c i j) -> p c j i", i=4, j=PACK),
+                              w2_raw[:].rearrange("p j (c i) -> p c j i", i=4))
+
+        at1 = tile("at1", [P, PACK, S], F32)
+        at2 = tile("at2", [P, PACK, S], F32)
+        top = tile("top", [P, PACK, S], F32, tag="w2_raw")
+        u = tile("u", [P, PACK, S], F32)
+        whole = slice(0, S)
+        last = PACK - 1
+
+        def look_up(dst, window, offsets, on_vector=False):
+            if on_vector:
+                nc.vector.tensor_copy(dst, window[:].indirect(offsets))
+            else:
+                nc.scalar.activation(dst, window[:].indirect(offsets), ACT.Copy)
+
+        for t in range(last):
+            look_up(at1[:, t, :], y_sb[t], l_n1[:])
+            look_up(at2[:, t, :], y_sb[t], l_n2[:], on_vector=(t == 0))
+        for h in range(2):
+            look_up(at1[:, last, cols(h)], y_sb[last], entries(l_n1, h))
+            look_up(at2[:, last, cols(h)], y_sb[last], entries(l_n2, h))
+
+        def larger(tiles, span):
+            nc.vector.tensor_tensor(top[:, tiles, span], at1[:, tiles, span], at2[:, tiles, span], ALU.max)
+
+        def less_own(t, span):
+            nc.vector.scalar_tensor_tensor(u[:, t, span], y_sb[t][:, span], -0.75, top[:, t, span], ALU.mult, ALU.add)
+
+        z_bf = [tile("z_bf%d" % h, [P, HALF * PACK], BF16) for h in range(2)]
+        z_w = [tile("z_w%d" % h, [P, HALF], U32) for h in range(2)]
+        z_s = [tile("z_s%d" % h, [P, HALF], U8) for h in range(2)]
         w2_w = tile("w2_w", [P, N], U32)
         w2_s = tile("w2_s", [P, N], U8)
+        a_acc = [psum.tile([P, S], F32, name="acc_a%d" % t, tag="bank%d" % t) for t in range(PACK)]
 
-        def quantise_w2():
-            w2_bf = tile("w2_bf", [P, N * PACK], BF16)
-            nc.vector.tensor_copy(w2_bf[:].rearrange("p (c i j) -> p c j i", i=4, j=PACK),
-                                  w2_raw[:].rearrange("p j (c i) -> p c j i", i=4))
-            nc.vector.quantize_mx(out=w2_w[:].bitcast(FP8X4), scales=w2_s[:], in_=w2_bf[:])
-
-        th = [tile("th%d" % t, [P, S], F32) for t in range(PACK)]
-        a_half = [tile("a_half%d" % t, [P, S], F32) for t in range(PACK)]
-
-        def make_z(h):
-            at1 = tile("at1_%d" % h, [P, PACK, HALF], F32)
-            at2 = tile("at2_%d" % h, [P, PACK, HALF], F32)
-            top = tile("top_%d" % h, [P, PACK, HALF], F32, tag="w2_raw" if h == 0 else None)
-            u = tile("u_%d" % h, [P, PACK, HALF], F32)
-            for t in range(PACK):
-                nc.scalar.activation(at1[:, t, :], y_sb[t][:].indirect(entries(l_n1, h)), ACT.Copy)
-                nc.scalar.activation(at2[:, t, :], y_sb[t][:].indirect(entries(l_n2, h)), ACT.Copy)
-                nc.vector.tensor_tensor(top[:, t, :], at1[:, t, :], at2[:, t, :], ALU.max)
-                nc.vector.scalar_tensor_tensor(u[:, t, :], y_sb[t][:, cols(h)], -0.75, top[:, t, :], ALU.mult, ALU.add)
-            z_bf = tile("z_bf%d" % h, [P, HALF * PACK], BF16)
+        def round_z(h):
             nc.vector.tensor_tensor(
-                z_bf[:].rearrange("p (c i t) -> p c t i", i=4, t=PACK),
-                u[:].rearrange("p t (c i) -> p c t i", i=4),
+                z_bf[h][:].rearrange("p (c i t) -> p c t i", i=4, t=PACK),
+                u[:, :, cols(h)].rearrange("p t (c i) -> p c t i", i=4),
                 gain[:].unsqueeze(1).unsqueeze(3).broadcast_to([P, HALF // 4, PACK, 4]),
                 ALU.mult,
             )
-            z_w = tile("z_w%d" % h, [P, HALF], U32)
-            z_s = tile("z_s%d" % h, [P, HALF], U8)
-            nc.vector.quantize_mx(out=z_w[:].bitcast(FP8X4), scales=z_s[:], in_=z_bf[:])
-            return z_w, z_s
 
-        def make_a(h, z_w, z_s):
-            for pair in range(2):
-                acc = psum.tile([P, 2, HALF], F32, name="acc_a%d_%d" % (h, pair), tag="bank%d" % (2 * h + pair))
-                for e in range(2):
-                    rows = slice((2 * pair + e) * P, (2 * pair + e + 1) * P)
-                    mx(acc[:, e, :], w2_w[:, rows], w2_s[:, rows], z_w[:], z_s[:])
-                for e in range(2):
-                    nc.scalar.activation(a_half[2 * pair + e][:, cols(h)], acc[:, e, :], ACT.Copy, scale=-0.5)
+        def multiply_z(h):
+            nc.vector.quantize_mx(out=z_w[h][:].bitcast(FP8X4), scales=z_s[h][:], in_=z_bf[h][:])
+            for t in range(PACK):
+                rows = slice(t * P, (t + 1) * P)
+                mx(a_acc[t][:, cols(h)], w2_w[:, rows], w2_s[:, rows], z_w[h][:], z_s[h][:])
 
-        quantise_w2()
-        z0 = make_z(0)
-        z1 = make_z(1)
+        larger(slice(0, 2), whole)
+        nc.vector.quantize_mx(out=w2_w[:].bitcast(FP8X4), scales=w2_s[:], in_=w2_bf[:])
+        less_own(0, whole)
+        less_own(1, whole)
+        larger(2, whole)
+        larger(last, cols(0))
+        less_own(2, whole)
+        less_own(last, cols(0))
+        larger(last, cols(1))
+        round_z(0)
+        less_own(last, cols(1))
+        multiply_z(0)
+        round_z(1)
+        multiply_z(1)
+
         for t in range(PACK):
-            nc.scalar.activation(th[t][:], b_acc[t][:], ACT.Tanh, scale=0.03125)
-        make_a(0, *z0)
-        make_a(1, *z1)
-        th4_first = tile("th4_first", [P, S], F32, tag="top_1")
-        th4_rest = tile("th4_rest", [P, PACK - 1, S], F32, tag="z_w1")
+            nc.scalar.activation(th[t][:, :S], b_acc[t][:], ACT.Tanh, scale=-0.03125)
         for t in range(PACK):
-            th4 = th4_first[:] if t == 0 else th4_rest[:, t - 1, :]
-            for h in range(2):
-                if t == 0:
-                    nc.vector.tensor_copy(th4[:, cols(h)], th[t][:].indirect(entries(l_n4, h)))
-                else:
-                    nc.scalar.activation(th4[:, cols(h)], th[t][:].indirect(entries(l_n4, h)), ACT.Copy)
-            neg = tile("neg%d" % t, [P, S], F32)
-            nc.vector.scalar_tensor_tensor(neg[:], th4, 1.0, a_half[t][:], ALU.add, ALU.mult)
-            res = tile("res%d" % t, [P, S], F32)
-            if t < PACK - 1:
-                for h in range(2):
-                    nc.vector.tensor_tensor(res[:, cols(h)], a_half[t][:].indirect(entries(l_n3, h)), neg[:, cols(h)], ALU.subtract)
-                nc.sync.dma_start(out[t * P : (t + 1) * P, :], res[:])
-            else:
-                at3 = tile("at3", [P, S], F32)
-                for h in range(2):
-                    nc.scalar.activation(at3[:, cols(h)], a_half[t][:].indirect(entries(l_n3, h)), ACT.Copy)
-                    nc.vector.tensor_tensor(res[:, cols(h)], at3[:, cols(h)], neg[:, cols(h)], ALU.subtract)
-                    nc.sync.dma_start(out[t * P : (t + 1) * P, cols(h)], res[:, cols(h)])
+            nc.scalar.activation(a_half[t][:, :S], a_acc[t][:], ACT.Copy, scale=-0.5)
+        held_by = {0: "u", last: "z_s1"}
+        th4 = [tile("th4_%d" % t, [P, S], F32, tag=held_by.get(t)) for t in range(PACK)]
+        for t in range(PACK):
+            look_up(th4[t][:], th[t], l_n4[:], on_vector=(t == 0))
+        at3 = tile("at3", [P, 2, S], F32)
+        look_up(at3[:, 0, :], a_half[2], l_n3[:])
+        for h in range(2):
+            look_up(at3[:, 1, cols(h)], a_half[last], entries(l_n3, h))
+
+        gated = tile("gated", [P, PACK, S], F32)
+
+        def gate(t):
+            nc.vector.scalar_tensor_tensor(gated[:, t, :], th4[t][:], -1.0, a_half[t][:, :S], ALU.add, ALU.mult)
+
+        def finish(t):
+            res = tile("res%d" % t, [P, S], F32, tag=(held_by.get(t + 1) or "th4_%d" % (t + 1)) if t < last else None)
+            rows = slice(t * P, (t + 1) * P)
+            if t < 2:
+                nc.vector.tensor_tensor(res[:], a_half[t][:].indirect(l_n3[:]), gated[:, t, :], ALU.add)
+            for span in ([whole] if t < last else [cols(0), cols(1)]):
+                if t >= 2:
+                    nc.vector.tensor_tensor(res[:, span], at3[:, t - 2, span], gated[:, t, span], ALU.add)
+                nc.sync.dma_start(out[rows, span], res[:, span])
+
+        gate(0)
+        for t in range(last):
+            gate(t + 1)
+            finish(t)
+        finish(last)

@@ -2,7 +2,7 @@ from contextlib import ExitStack
 
 import concourse.mybir as mybir
 
-K, T, S, N, H, G = 512, 2048, 512, 512, 512, 2048
+T, S, N, H, G = 2048, 512, 512, 512, 2048
 FLOPS = 3 * 2 * 512 * 512 * 512
 
 F32 = mybir.dt.float32
@@ -17,10 +17,14 @@ ACT = mybir.ActivationFunctionType
 
 P = 128
 PACK = 4
+QUADRANTS = 4
+LINE = 4
 HALF = S // 2
 LIST_COLS = S // 16
-S_WINDOW = S + 16
-V_WINDOW = S + 192
+EIGHT_LIST_WINDOW = 2 * S
+COPY_WINDOW = S + 192
+NARROW_WINDOW = S + 16
+FUSED_TILES = 2
 
 
 def tile_picked_cdjoingatebover_none_p_kernel(
@@ -45,29 +49,47 @@ def tile_picked_cdjoingatebover_none_p_kernel(
         def entries(held, h):
             return held[:, h * HALF // 16 : (h + 1) * HALF // 16]
 
+        def rows(t):
+            return slice(t * P, (t + 1) * P)
+
+        def scale_rows(q):
+            return slice(32 * q, 32 * q + 4)
+
         def mx(acc, lhs_w, lhs_s, rhs_w, rhs_s):
-            nc.tensor.matmul_mx(out=acc, lhsT=lhs_w.bitcast(FP8X4), lhsT_scale=lhs_s,
-                                rhs=rhs_w.bitcast(FP8X4), rhs_scale=rhs_s, start=True, stop=True)
+            nc.tensor.matmul_mx(
+                out=acc,
+                lhsT=lhs_w.bitcast(FP8X4),
+                lhsT_scale=lhs_s,
+                rhs=rhs_w.bitcast(FP8X4),
+                rhs_scale=rhs_s,
+                start=True,
+                stop=True,
+            )
+
+        def look_up(dst, window, offsets, on_vector=False):
+            if on_vector:
+                nc.vector.tensor_copy(dst, window[:].indirect(offsets))
+            else:
+                nc.scalar.activation(dst, window[:].indirect(offsets), ACT.Copy)
 
         xs = tile("xs", [P, T], U8)
         ds = tile("ds", [P, G], U8)
         dk_s = tile("dk_s", [P, H], U8)
         xs_in = tile("xs_in", [P, T], U8)
-        nc.vector.memset(ds[:].bitcast(I32), 0)
         nc.vector.memset(xs[:].bitcast(I32), 0)
-        nc.gpsimd.dma_start(ds[0:P:8, :].bitcast(I32), d_scales[0].bitcast(I32))
+        nc.vector.memset(ds[:].bitcast(I32), 0)
         nc.vector.memset(dk_s[:].bitcast(I32), 0)
-        y_sb = [tile("y%d" % t, [P, 2 * S], F32) for t in range(PACK)]
-        th = [tile("th%d" % t, [P, V_WINDOW if t == 0 else S_WINDOW], F32) for t in range(PACK)]
-        a_half = [tile("a_half%d" % t, [P, S_WINDOW], F32) for t in range(PACK)]
+        y_sb = [tile("y%d" % t, [P, EIGHT_LIST_WINDOW], F32) for t in range(PACK)]
+        gate = [tile("gate%d" % t, [P, COPY_WINDOW if t == 0 else NARROW_WINDOW], F32) for t in range(PACK)]
+        a_half = [tile("a_half%d" % t, [P, NARROW_WINDOW], F32) for t in range(PACK)]
         for window in y_sb:
             nc.vector.memset(window[:, S:], 0.0)
-        for window in th + a_half:
+        for window in gate + a_half:
             nc.gpsimd.memset(window[:, S:], 0.0)
 
         l_offs = load_list("l_offs", offs)
-        for q in range(4):
-            nc.sync.dma_start(xs_in[32 * q : 32 * q + 4, :].bitcast(I32), x_scales[0, 4 * q : 4 * q + 4, :].bitcast(I32))
+        for q in range(QUADRANTS):
+            nc.sync.dma_start(xs_in[scale_rows(q), :].bitcast(I32), x_scales[0, 4 * q : 4 * q + 4, :].bitcast(I32))
         w1_raw = tile("w1_raw", [P, PACK, H], F32)
         nc.sync.dma_start(w1_raw[:], w1.rearrange("(p j) c -> p j c", j=PACK))
         xw = tile("xw", [P, T], U32)
@@ -77,67 +99,63 @@ def tile_picked_cdjoingatebover_none_p_kernel(
         l_n1 = load_list("l_n1", n1)
         l_n2 = load_list("l_n2", n2)
         l_n4 = load_list("l_n4", n4)
-        l_n3 = load_list("l_n3", n3)
-        dw = tile("dw", [P, G], U32)
-        nc.sync.dma_start(dw[:].bitcast(I32), d_words[0].rearrange("p n t -> p (n t)").bitcast(I32))
-        w2_raw = tile("w2_raw", [P, PACK, N], F32)
-        nc.sync.dma_start(w2_raw[:], w2.rearrange("(p j) c -> p j c", j=PACK))
         gain = tile("gain", [P, PACK], F32)
         nc.sync.dma_start(gain[:], gn.rearrange("(p t) o -> p (t o)", t=PACK))
+        dw = tile("dw", [P, G], U32)
+        nc.sync.dma_start(dw[:].bitcast(I32), d_words[0].rearrange("p n t -> p (n t)").bitcast(I32))
+        l_n3 = load_list("l_n3", n3)
+        nc.sync.dma_start(ds[0:P:8, :].bitcast(I32), d_scales[0].bitcast(I32))
 
-        for q in range(4):
-            nc.vector.tensor_copy(xs[32 * q : 32 * q + 4, :].bitcast(I32), xs_in[32 * q : 32 * q + 4, :].bitcast(I32))
+        for q in range(QUADRANTS):
+            nc.vector.tensor_copy(xs[scale_rows(q), :].bitcast(I32), xs_in[scale_rows(q), :].bitcast(I32))
         xq_s = tile("xq_s", [P, S], U8)
         nc.vector.tensor_copy(xq_s[:], xs[:].indirect(l_offs[:]))
-        w1_bf = tile("w1_bf", [P, PACK * P * PACK], BF16)
+        w1_bf = tile("w1_bf", [P, H * PACK], BF16)
         w1_dst = w1_bf[:].rearrange("p (t m j) -> p m j t", t=PACK, j=PACK)
         w1_src = w1_raw[:].rearrange("p j (m t) -> p m j t", t=PACK)
         nc.scalar.copy(w1_dst[:, : P // 2], w1_src[:, : P // 2])
         nc.vector.tensor_copy(w1_dst[:, P // 2 :], w1_src[:, P // 2 :])
+        w2_raw = tile("w2_raw", [P, PACK, N], F32, tag="w1_raw")
+        nc.sync.dma_start(w2_raw[:], w2.rearrange("(p j) c -> p j c", j=PACK))
         w1_w = tile("w1_w", [P, H], U32)
         w1_s = tile("w1_s", [P, H], U8)
         nc.vector.quantize_mx(out=w1_w[:].bitcast(FP8X4), scales=w1_s[:], in_=w1_bf[:])
         xq_w = tile("xq_w", [P, S], U32)
         nc.vector.tensor_copy(xq_w[:], xw[:].indirect(l_offs[:]))
         for t in range(PACK):
-            acc = psum.tile([P, S], F32, name="acc_y%d" % t, tag="bank%d" % t)
-            rows = slice(t * P, (t + 1) * P)
-            mx(acc[:], w1_w[:, rows], w1_s[:, rows], xq_w[:], xq_s[:])
-            nc.scalar.copy(y_sb[t][:, :S], acc[:])
+            y_acc = psum.tile([P, S], F32, name="y_acc%d" % t, tag="bank%d" % t)
+            mx(y_acc[:], w1_w[:, rows(t)], w1_s[:, rows(t)], xq_w[:], xq_s[:])
+            nc.scalar.copy(y_sb[t][:, :S], y_acc[:])
 
         x2_s = tile("x2_s", [P, S], U8)
         nc.vector.tensor_copy(x2_s[:], xs[:].indirect(l_two[:]))
         dk_g = tile("dk_g", [P, H], U8)
         nc.vector.tensor_copy(dk_g[:], ds[:].indirect(l_k1[:]))
-        for q in range(4):
-            nc.sync.dma_start(dk_s[32 * q : 32 * q + 4, :].bitcast(I32), dk_g[32 * q : 32 * q + 32 : 8, :].bitcast(I32))
+        for q in range(QUADRANTS):
+            nc.sync.dma_start(dk_s[scale_rows(q), :].bitcast(I32), dk_g[32 * q : 32 * q + 32 : 8, :].bitcast(I32))
         x2_w = tile("x2_w", [P, S], U32)
         nc.vector.tensor_copy(x2_w[:], xw[:].indirect(l_two[:]))
         dk_w = tile("dk_w", [P, H], U32)
         nc.vector.tensor_copy(dk_w[:], dw[:].indirect(l_k1[:]))
-        b_acc = []
+        b_acc = [psum.tile([P, S], F32, name="b_acc%d" % t, tag="bank%d" % (PACK + t)) for t in range(PACK)]
         for t in range(PACK):
-            acc = psum.tile([P, S], F32, name="acc_b%d" % t, tag="bank%d" % (PACK + t))
-            rows = slice(t * P, (t + 1) * P)
-            mx(acc[:], dk_w[:, rows], dk_s[:, rows], x2_w[:], x2_s[:])
-            b_acc.append(acc)
+            mx(b_acc[t][:], dk_w[:, rows(t)], dk_s[:, rows(t)], x2_w[:], x2_s[:])
 
         w2_bf = tile("w2_bf", [P, N * PACK], BF16)
-        nc.vector.tensor_copy(w2_bf[:].rearrange("p (c i j) -> p c j i", i=4, j=PACK),
-                              w2_raw[:].rearrange("p j (c i) -> p c j i", i=4))
+        nc.vector.tensor_copy(
+            w2_bf[:].rearrange("p (c i j) -> p c j i", i=LINE, j=PACK),
+            w2_raw[:].rearrange("p j (c i) -> p c j i", i=LINE),
+        )
 
         at1 = tile("at1", [P, PACK, S], F32)
         at2 = tile("at2", [P, PACK, S], F32)
-        top = tile("top", [P, PACK, S], F32, tag="w2_raw")
-        u = tile("u", [P, PACK, S], F32)
+        top = tile("top", [P, PACK, S], F32, tag="w1_raw")
+        z = tile("z", [P, PACK, S], F32)
+        own = tile("own", [P, PACK, S], F32)
+        for t in range(PACK):
+            nc.vector.tensor_scalar(own[:, t, :], y_sb[t][:, :S], gain[:, t : t + 1], -0.75, ALU.mult, ALU.mult)
         whole = slice(0, S)
         last = PACK - 1
-
-        def look_up(dst, window, offsets, on_vector=False):
-            if on_vector:
-                nc.vector.tensor_copy(dst, window[:].indirect(offsets))
-            else:
-                nc.scalar.activation(dst, window[:].indirect(offsets), ACT.Copy)
 
         for t in range(last):
             look_up(at1[:, t, :], y_sb[t], l_n1[:])
@@ -149,75 +167,75 @@ def tile_picked_cdjoingatebover_none_p_kernel(
         def larger(tiles, span):
             nc.vector.tensor_tensor(top[:, tiles, span], at1[:, tiles, span], at2[:, tiles, span], ALU.max)
 
-        def less_own(t, span):
-            nc.vector.scalar_tensor_tensor(u[:, t, span], y_sb[t][:, span], -0.75, top[:, t, span], ALU.mult, ALU.add)
+        def make_z(t, span):
+            nc.vector.scalar_tensor_tensor(
+                z[:, t, span], top[:, t, span], gain[:, t : t + 1], own[:, t, span], ALU.mult, ALU.add
+            )
 
         z_bf = [tile("z_bf%d" % h, [P, HALF * PACK], BF16) for h in range(2)]
         z_w = [tile("z_w%d" % h, [P, HALF], U32) for h in range(2)]
         z_s = [tile("z_s%d" % h, [P, HALF], U8) for h in range(2)]
         w2_w = tile("w2_w", [P, N], U32)
         w2_s = tile("w2_s", [P, N], U8)
-        a_acc = [psum.tile([P, S], F32, name="acc_a%d" % t, tag="bank%d" % t) for t in range(PACK)]
+        a_acc = [psum.tile([P, S], F32, name="a_acc%d" % t, tag="bank%d" % t) for t in range(PACK)]
 
         def round_z(h):
-            nc.vector.tensor_tensor(
-                z_bf[h][:].rearrange("p (c i t) -> p c t i", i=4, t=PACK),
-                u[:, :, cols(h)].rearrange("p t (c i) -> p c t i", i=4),
-                gain[:].unsqueeze(1).unsqueeze(3).broadcast_to([P, HALF // 4, PACK, 4]),
-                ALU.mult,
+            nc.vector.tensor_copy(
+                z_bf[h][:].rearrange("p (c i t) -> p c t i", i=LINE, t=PACK),
+                z[:, :, cols(h)].rearrange("p t (c i) -> p c t i", i=LINE),
             )
 
         def multiply_z(h):
             nc.vector.quantize_mx(out=z_w[h][:].bitcast(FP8X4), scales=z_s[h][:], in_=z_bf[h][:])
             for t in range(PACK):
-                rows = slice(t * P, (t + 1) * P)
-                mx(a_acc[t][:, cols(h)], w2_w[:, rows], w2_s[:, rows], z_w[h][:], z_s[h][:])
+                mx(a_acc[t][:, cols(h)], w2_w[:, rows(t)], w2_s[:, rows(t)], z_w[h][:], z_s[h][:])
 
         larger(slice(0, 2), whole)
         nc.vector.quantize_mx(out=w2_w[:].bitcast(FP8X4), scales=w2_s[:], in_=w2_bf[:])
-        less_own(0, whole)
-        less_own(1, whole)
+        make_z(0, whole)
+        make_z(1, whole)
         larger(2, whole)
         larger(last, cols(0))
-        less_own(2, whole)
-        less_own(last, cols(0))
+        make_z(2, whole)
+        make_z(last, cols(0))
         larger(last, cols(1))
         round_z(0)
-        less_own(last, cols(1))
+        make_z(last, cols(1))
         multiply_z(0)
         round_z(1)
         multiply_z(1)
 
         for t in range(PACK):
-            nc.scalar.activation(th[t][:, :S], b_acc[t][:], ACT.Tanh, scale=-0.03125)
+            nc.scalar.activation(gate[t][:, :S], b_acc[t][:], ACT.Tanh, scale=-0.03125)
         for t in range(PACK):
             nc.scalar.activation(a_half[t][:, :S], a_acc[t][:], ACT.Copy, scale=-0.5)
-        held_by = {0: "u", last: "z_s1"}
-        th4 = [tile("th4_%d" % t, [P, S], F32, tag=held_by.get(t)) for t in range(PACK)]
+        gate4_tags = ["z", "gate4_1", "gate4_2", "z_s1"]
+        gate4 = [tile("gate4_%d" % t, [P, S], F32, tag=gate4_tags[t]) for t in range(PACK)]
         for t in range(PACK):
-            look_up(th4[t][:], th[t], l_n4[:], on_vector=(t == 0))
-        at3 = tile("at3", [P, 2, S], F32)
-        look_up(at3[:, 0, :], a_half[2], l_n3[:])
+            look_up(gate4[t][:], gate[t], l_n4[:], on_vector=(t == 0))
+        spans = [[whole] if t < last else [cols(0), cols(1)] for t in range(PACK)]
+        at3 = tile("at3", [P, PACK - FUSED_TILES, S], F32)
+        look_up(at3[:, 0, :], a_half[FUSED_TILES], l_n3[:])
         for h in range(2):
-            look_up(at3[:, 1, cols(h)], a_half[last], entries(l_n3, h))
+            look_up(at3[:, last - FUSED_TILES, cols(h)], a_half[last], entries(l_n3, h))
 
         gated = tile("gated", [P, PACK, S], F32)
 
-        def gate(t):
-            nc.vector.scalar_tensor_tensor(gated[:, t, :], th4[t][:], -1.0, a_half[t][:, :S], ALU.add, ALU.mult)
+        def apply_gate(t):
+            nc.vector.scalar_tensor_tensor(gated[:, t, :], gate4[t][:], -1.0, a_half[t][:, :S], ALU.add, ALU.mult)
 
         def finish(t):
-            res = tile("res%d" % t, [P, S], F32, tag=(held_by.get(t + 1) or "th4_%d" % (t + 1)) if t < last else None)
-            rows = slice(t * P, (t + 1) * P)
-            if t < 2:
-                nc.vector.tensor_tensor(res[:], a_half[t][:].indirect(l_n3[:]), gated[:, t, :], ALU.add)
-            for span in ([whole] if t < last else [cols(0), cols(1)]):
-                if t >= 2:
-                    nc.vector.tensor_tensor(res[:, span], at3[:, t - 2, span], gated[:, t, span], ALU.add)
-                nc.sync.dma_start(out[rows, span], res[:, span])
+            res = tile("res%d" % t, [P, S], F32, tag=gate4_tags[t + 1] if t < last else None)
+            for span in spans[t]:
+                if t < FUSED_TILES:
+                    fetched = a_half[t][:].indirect(l_n3[:])
+                else:
+                    fetched = at3[:, t - FUSED_TILES, span]
+                nc.vector.tensor_tensor(res[:, span], fetched, gated[:, t, span], ALU.add)
+                nc.sync.dma_start(out[rows(t), span], res[:, span])
 
-        gate(0)
+        apply_gate(0)
         for t in range(last):
-            gate(t + 1)
+            apply_gate(t + 1)
             finish(t)
         finish(last)

from contextlib import ExitStack

import concourse.mybir as mybir

T, S, N, H, G = 2048, 512, 512, 512, 2048
FLOPS = 3 * 2 * 512 * 512 * 512

F32 = mybir.dt.float32
BF16 = mybir.dt.bfloat16
I32 = mybir.dt.int32
U32 = mybir.dt.uint32
U16 = mybir.dt.uint16
U8 = mybir.dt.uint8
FP8X4 = mybir.dt.float8_e4m3fn_x4
ALU = mybir.AluOpType
ACT = mybir.ActivationFunctionType

P = 128
PACK = 4
QUADRANTS = 4
LINE = 4
HALF = S // 2
LIST_COLS = S // 16
EIGHT_LIST_WINDOW = 2 * S
COPY_WINDOW = S + 192
NARROW_WINDOW = S + 16
FUSED_TILES = 2


def tile_picked_cdjoingatebover_none_p_kernel(
    tc, x_words, x_scales, w1, gn, w2, d_words, d_scales, offs, n1, n2, two, k1, n3, n4, out
):
    nc = tc.nc
    with ExitStack() as ctx:
        keep = ctx.enter_context(tc.tile_pool(name="keep", bufs=1))
        psum = ctx.enter_context(tc.psum_pool(name="psum", bufs=1))

        def tile(name, shape, dtype, tag=None):
            return keep.tile(shape, dtype, name=name, tag=tag or name, align_bytes=64)

        def load_list(name, src):
            held = tile(name, [P, LIST_COLS], U16)
            nc.sync.dma_start(held[:], src)
            return held

        def cols(h):
            return slice(h * HALF, (h + 1) * HALF)

        def entries(held, h):
            return held[:, h * HALF // 16 : (h + 1) * HALF // 16]

        def rows(t):
            return slice(t * P, (t + 1) * P)

        def scale_rows(q):
            return slice(32 * q, 32 * q + 4)

        def mx(acc, lhs_w, lhs_s, rhs_w, rhs_s):
            nc.tensor.matmul_mx(
                out=acc,
                lhsT=lhs_w.bitcast(FP8X4),
                lhsT_scale=lhs_s,
                rhs=rhs_w.bitcast(FP8X4),
                rhs_scale=rhs_s,
                start=True,
                stop=True,
            )

        def look_up(dst, window, offsets, on_vector=False):
            if on_vector:
                nc.vector.tensor_copy(dst, window[:].indirect(offsets))
            else:
                nc.scalar.activation(dst, window[:].indirect(offsets), ACT.Copy)

        xs = tile("xs", [P, T], U8)
        ds = tile("ds", [P, G], U8)
        dk_s = tile("dk_s", [P, H], U8)
        xs_in = tile("xs_in", [P, T], U8)
        nc.vector.memset(xs[:].bitcast(I32), 0)
        nc.vector.memset(ds[:].bitcast(I32), 0)
        nc.vector.memset(dk_s[:].bitcast(I32), 0)
        y_sb = [tile("y%d" % t, [P, EIGHT_LIST_WINDOW], F32) for t in range(PACK)]
        gate = [tile("gate%d" % t, [P, COPY_WINDOW if t == 0 else NARROW_WINDOW], F32) for t in range(PACK)]
        a_half = [tile("a_half%d" % t, [P, NARROW_WINDOW], F32) for t in range(PACK)]
        for window in y_sb:
            nc.vector.memset(window[:, S:], 0.0)
        for window in gate + a_half:
            nc.gpsimd.memset(window[:, S:], 0.0)

        l_offs = load_list("l_offs", offs)
        for q in range(QUADRANTS):
            nc.sync.dma_start(xs_in[scale_rows(q), :].bitcast(I32), x_scales[0, 4 * q : 4 * q + 4, :].bitcast(I32))
        w1_raw = tile("w1_raw", [P, PACK, H], F32)
        nc.sync.dma_start(w1_raw[:], w1.rearrange("(p j) c -> p j c", j=PACK))
        xw = tile("xw", [P, T], U32)
        nc.sync.dma_start(xw[:].bitcast(I32), x_words[0].rearrange("p n t -> p (n t)").bitcast(I32))
        l_two = load_list("l_two", two)
        l_k1 = load_list("l_k1", k1)
        l_n1 = load_list("l_n1", n1)
        l_n2 = load_list("l_n2", n2)
        l_n4 = load_list("l_n4", n4)
        gain = tile("gain", [P, PACK], F32)
        nc.sync.dma_start(gain[:], gn.rearrange("(p t) o -> p (t o)", t=PACK))
        dw = tile("dw", [P, G], U32)
        nc.sync.dma_start(dw[:].bitcast(I32), d_words[0].rearrange("p n t -> p (n t)").bitcast(I32))
        l_n3 = load_list("l_n3", n3)
        nc.sync.dma_start(ds[0:P:8, :].bitcast(I32), d_scales[0].bitcast(I32))

        for q in range(QUADRANTS):
            nc.vector.tensor_copy(xs[scale_rows(q), :].bitcast(I32), xs_in[scale_rows(q), :].bitcast(I32))
        xq_s = tile("xq_s", [P, S], U8)
        nc.vector.tensor_copy(xq_s[:], xs[:].indirect(l_offs[:]))
        w1_bf = tile("w1_bf", [P, H * PACK], BF16)
        w1_dst = w1_bf[:].rearrange("p (t m j) -> p m j t", t=PACK, j=PACK)
        w1_src = w1_raw[:].rearrange("p j (m t) -> p m j t", t=PACK)
        nc.scalar.copy(w1_dst[:, : P // 2], w1_src[:, : P // 2])
        nc.vector.tensor_copy(w1_dst[:, P // 2 :], w1_src[:, P // 2 :])
        w2_raw = tile("w2_raw", [P, PACK, N], F32, tag="w1_raw")
        nc.sync.dma_start(w2_raw[:], w2.rearrange("(p j) c -> p j c", j=PACK))
        w1_w = tile("w1_w", [P, H], U32)
        w1_s = tile("w1_s", [P, H], U8)
        nc.vector.quantize_mx(out=w1_w[:].bitcast(FP8X4), scales=w1_s[:], in_=w1_bf[:])
        xq_w = tile("xq_w", [P, S], U32)
        nc.vector.tensor_copy(xq_w[:], xw[:].indirect(l_offs[:]))
        for t in range(PACK):
            y_acc = psum.tile([P, S], F32, name="y_acc%d" % t, tag="bank%d" % t)
            mx(y_acc[:], w1_w[:, rows(t)], w1_s[:, rows(t)], xq_w[:], xq_s[:])
            nc.scalar.copy(y_sb[t][:, :S], y_acc[:])

        x2_s = tile("x2_s", [P, S], U8)
        nc.vector.tensor_copy(x2_s[:], xs[:].indirect(l_two[:]))
        dk_g = tile("dk_g", [P, H], U8)
        nc.vector.tensor_copy(dk_g[:], ds[:].indirect(l_k1[:]))
        for q in range(QUADRANTS):
            nc.sync.dma_start(dk_s[scale_rows(q), :].bitcast(I32), dk_g[32 * q : 32 * q + 32 : 8, :].bitcast(I32))
        x2_w = tile("x2_w", [P, S], U32)
        nc.vector.tensor_copy(x2_w[:], xw[:].indirect(l_two[:]))
        dk_w = tile("dk_w", [P, H], U32)
        nc.vector.tensor_copy(dk_w[:], dw[:].indirect(l_k1[:]))
        b_acc = [psum.tile([P, S], F32, name="b_acc%d" % t, tag="bank%d" % (PACK + t)) for t in range(PACK)]
        for t in range(PACK):
            mx(b_acc[t][:], dk_w[:, rows(t)], dk_s[:, rows(t)], x2_w[:], x2_s[:])

        w2_bf = tile("w2_bf", [P, N * PACK], BF16)
        nc.vector.tensor_copy(
            w2_bf[:].rearrange("p (c i j) -> p c j i", i=LINE, j=PACK),
            w2_raw[:].rearrange("p j (c i) -> p c j i", i=LINE),
        )

        at1 = tile("at1", [P, PACK, S], F32)
        at2 = tile("at2", [P, PACK, S], F32)
        top = tile("top", [P, PACK, S], F32, tag="w1_raw")
        z = tile("z", [P, PACK, S], F32)
        own = tile("own", [P, PACK, S], F32)
        for t in range(PACK):
            nc.vector.tensor_scalar(own[:, t, :], y_sb[t][:, :S], gain[:, t : t + 1], -0.75, ALU.mult, ALU.mult)
        whole = slice(0, S)
        last = PACK - 1

        for t in range(last):
            look_up(at1[:, t, :], y_sb[t], l_n1[:])
            look_up(at2[:, t, :], y_sb[t], l_n2[:], on_vector=(t == 0))
        for h in range(2):
            look_up(at1[:, last, cols(h)], y_sb[last], entries(l_n1, h))
            look_up(at2[:, last, cols(h)], y_sb[last], entries(l_n2, h))

        def larger(tiles, span):
            nc.vector.tensor_tensor(top[:, tiles, span], at1[:, tiles, span], at2[:, tiles, span], ALU.max)

        def make_z(t, span):
            nc.vector.scalar_tensor_tensor(
                z[:, t, span], top[:, t, span], gain[:, t : t + 1], own[:, t, span], ALU.mult, ALU.add
            )

        z_bf = [tile("z_bf%d" % h, [P, HALF * PACK], BF16) for h in range(2)]
        z_w = [tile("z_w%d" % h, [P, HALF], U32) for h in range(2)]
        z_s = [tile("z_s%d" % h, [P, HALF], U8) for h in range(2)]
        w2_w = tile("w2_w", [P, N], U32)
        w2_s = tile("w2_s", [P, N], U8)
        a_acc = [psum.tile([P, S], F32, name="a_acc%d" % t, tag="bank%d" % t) for t in range(PACK)]

        def round_z(h):
            nc.vector.tensor_copy(
                z_bf[h][:].rearrange("p (c i t) -> p c t i", i=LINE, t=PACK),
                z[:, :, cols(h)].rearrange("p t (c i) -> p c t i", i=LINE),
            )

        def multiply_z(h):
            nc.vector.quantize_mx(out=z_w[h][:].bitcast(FP8X4), scales=z_s[h][:], in_=z_bf[h][:])
            for t in range(PACK):
                mx(a_acc[t][:, cols(h)], w2_w[:, rows(t)], w2_s[:, rows(t)], z_w[h][:], z_s[h][:])

        larger(slice(0, 2), whole)
        nc.vector.quantize_mx(out=w2_w[:].bitcast(FP8X4), scales=w2_s[:], in_=w2_bf[:])
        make_z(0, whole)
        make_z(1, whole)
        larger(2, whole)
        larger(last, cols(0))
        make_z(2, whole)
        make_z(last, cols(0))
        larger(last, cols(1))
        round_z(0)
        make_z(last, cols(1))
        multiply_z(0)
        round_z(1)
        multiply_z(1)

        for t in range(PACK):
            nc.scalar.activation(gate[t][:, :S], b_acc[t][:], ACT.Tanh, scale=-0.03125)
        for t in range(PACK):
            nc.scalar.activation(a_half[t][:, :S], a_acc[t][:], ACT.Copy, scale=-0.5)
        gate4_tags = ["z", "gate4_1", "gate4_2", "z_s1"]
        gate4 = [tile("gate4_%d" % t, [P, S], F32, tag=gate4_tags[t]) for t in range(PACK)]
        for t in range(PACK):
            look_up(gate4[t][:], gate[t], l_n4[:], on_vector=(t == 0))
        spans = [[whole] if t < last else [cols(0), cols(1)] for t in range(PACK)]
        at3 = tile("at3", [P, PACK - FUSED_TILES, S], F32)
        look_up(at3[:, 0, :], a_half[FUSED_TILES], l_n3[:])
        for h in range(2):
            look_up(at3[:, last - FUSED_TILES, cols(h)], a_half[last], entries(l_n3, h))

        gated = tile("gated", [P, PACK, S], F32)

        def apply_gate(t):
            nc.vector.scalar_tensor_tensor(gated[:, t, :], gate4[t][:], -1.0, a_half[t][:, :S], ALU.add, ALU.mult)

        def finish(t):
            res = tile("res%d" % t, [P, S], F32, tag=gate4_tags[t + 1] if t < last else None)
            for span in spans[t]:
                if t < FUSED_TILES:
                    fetched = a_half[t][:].indirect(l_n3[:])
                else:
                    fetched = at3[:, t - FUSED_TILES, span]
                nc.vector.tensor_tensor(res[:, span], fetched, gated[:, t, span], ALU.add)
                nc.sync.dma_start(out[rows(t), span], res[:, span])

        apply_gate(0)
        for t in range(last):
            apply_gate(t + 1)
            finish(t)
        finish(last)
